import numpy as np
import ml_dtypes


def mxq(x, axis, fmt="e4m3"):
    dtype, down = {"e4m3": (ml_dtypes.float8_e4m3fn, 7), "e5m2": (ml_dtypes.float8_e5m2, 14)}[fmt]
    v = np.moveaxis(np.asarray(x, np.float32).astype(ml_dtypes.bfloat16).astype(np.float64), axis, -1)
    blocks = v.reshape(v.shape[:-1] + (-1, 32))
    amax = np.abs(blocks).max(-1, keepdims=True)
    byte = np.maximum(np.where(amax > 0, np.frexp(amax)[1] - 1 + 127, 0) - down, 1)
    scale = np.exp2(byte - 127.0)
    codes = (blocks / scale).astype(np.float32).astype(dtype).astype(np.float64)
    return np.moveaxis((codes * scale).reshape(v.shape), -1, axis)


WIDE = False


def mx_kscale(k):
    if not WIDE:
        return np.ones(k)
    levels = np.array([10, -10, 5, -5, 0])
    if k % 512:
        return np.exp2(np.random.permutation(np.resize(levels, k // 32))).repeat(32)
    a = np.empty((k // 512, 16))
    for p in range(k // 512):
        a[p, :8] = np.random.permutation(np.resize(levels, 8))
        for g in range(8):
            far = levels[np.abs(levels - a[p, g]) >= 10]
            a[p, g + 8] = far[np.random.randint(len(far))]
    return np.exp2(a.ravel()).repeat(32)


def f64(x):
    return np.asarray(x).astype(np.float64)


def striped(idx):
    return np.tile(np.asarray(idx).reshape(-1, 16).T, (8, 1)).astype(np.uint16)


def unstriped(offs):
    return offs[:16].T.reshape(-1).astype(np.int64)


E2M1 = np.array([0.0, 0.5, 1.0, 1.5, 2.0, 3.0, 4.0, 6.0, -0.0, -0.5, -1.0, -1.5, -2.0, -3.0, -4.0, -6.0])


def pack_weight(w, fmt):
    k, n = w.shape
    w = f64(np.asarray(w, np.float32).astype(ml_dtypes.bfloat16)).reshape(k // 32, 32, n)
    amax = np.abs(w).max(1)
    if fmt == "e4m3":
        byte = np.frexp(amax)[1] - 1 + 127 - 7
    else:
        mant, ex = np.frexp(amax / 6.0)
        byte = np.where(mant > 0.5, ex, ex - 1) + 127
    byte = np.clip(np.where(amax > 0, byte, 1), 1, 254)
    scaled = (w * np.exp2(127.0 - byte)[:, None, :]).reshape(k, n).astype(np.float32)
    by_word = np.ascontiguousarray(scaled.reshape(k // 512, 128, 4, n).transpose(0, 1, 3, 2))
    if fmt == "e4m3":
        words = by_word.astype(ml_dtypes.float8_e4m3fn).view(np.uint8)
    else:
        c = by_word.astype(ml_dtypes.float4_e2m1fn).view(np.uint8) & 0xF
        words = (c[..., 0::2] | (c[..., 1::2] << 4)).reshape(k // 512, 128, 2 * n)
    return np.ascontiguousarray(words), np.ascontiguousarray(byte.astype(np.uint8).reshape(k // 512, 16, n))


def unpack_weight(words, scales, fmt):
    g, _, n = scales.shape
    words = np.ascontiguousarray(words).reshape(g, 128, n, -1)
    if fmt == "e4m3":
        vals = words.view(ml_dtypes.float8_e4m3fn).astype(np.float64)
    else:
        nib = np.empty((g, 128, n, 4), np.uint8)
        nib[..., 0::2] = words & 0xF
        nib[..., 1::2] = words >> 4
        vals = E2M1[nib]
    vals = vals * np.repeat(np.exp2(scales.astype(np.float64) - 127.0), 8, axis=1)[..., None]
    return vals.transpose(0, 1, 3, 2).reshape(g * 512, n)


def sigmoid(v):
    return 1.0 / (1.0 + np.exp(-v))


K, R, F, T, J, G = 512, 128, 512, 2048, 512, 32


def setup_inputs():
    n = np.random.standard_normal
    idx = np.random.permutation(T)[:J]
    fk = mx_kscale(K)
    ff = mx_kscale(F)
    fj = mx_kscale(J)
    tj = np.ones(T)
    tj[idx] = fj
    tabp = pack_weight(n((K, T)) / fk[:, None], "e2m1")
    return {
        "tab_words": tabp[0],
        "tab_scales": tabp[1],
        "w1": (n((K, R)) * 1 / np.sqrt(K) * fk[:, None]).astype(np.float32),
        "steep": (np.random.uniform(1.0, 4.0, (R, 1))).astype(np.float32),
        "bias": (np.random.uniform(-0.5, 0.5, (R, 1))).astype(np.float32),
        "wo": (n((F, R)) * 1 / np.sqrt(F) * ff[:, None]).astype(np.float32),
        "dy": (n((F, J)) / ff[:, None]).astype(np.float32),
        "js": (np.random.uniform(0.5, 2.0, (1, J)) * fj).astype(np.float32),
        "xrows": (n((K, T)) / tj).astype(np.float32),
        "old": (n((K, R)) * 4.0).astype(np.float32),
        "offs": striped(idx),
    }


def reference(tab_words, tab_scales, w1, steep, bias, wo, dy, js, xrows, old, offs):
    idx = unstriped(offs)
    tabu = unpack_weight(tab_words, tab_scales, "e2m1")
    w1q = mxq(f64(w1), 0, "e4m3")
    tabidxg = tabu[:, idx]
    a = w1q.T @ tabidxg
    m1 = a.reshape(R, G, J // G).mean(axis=2)
    gt = sigmoid(m1 * f64(steep) + f64(bias))
    gr0 = np.repeat(gt, J // G, axis=1)
    woq = mxq(f64(wo), 0, "e4m3")
    dyq = mxq(f64(dy), 0, "e4m3")
    c0 = woq.T @ dyq
    dgr0 = c0 * a
    dgt = dgr0.reshape(R, G, J // G).sum(axis=2)
    dm1 = dgt * gt * (1.0 - gt) * f64(steep)
    e1 = dm1 / 16.0
    r1 = np.repeat(e1, J // G, axis=1)
    da = c0 * gr0 + r1
    gs = da * f64(js)
    gt1 = gs.T
    xt = f64(xrows)[:, idx].T
    xtq = mxq(xt, 0, "e4m3")
    gt1q = mxq(gt1, 0, "e4m3")
    gw = xtq.T @ gt1q
    y = gw + f64(old)
    return y

@@ -1,0 +1,185 @@
+from contextlib import ExitStack
+
+import concourse.mybir as mybir
+from concourse.masks import make_identity
+
+K, R, F, T, J, G = 512, 128, 512, 2048, 512, 32
+P = 128
+PACK = 4
+GROUP = J // G
+FLOPS = 2 * R * J * K + 2 * R * J * F + 2 * K * R * J
+
+F32 = mybir.dt.float32
+BF16 = mybir.dt.bfloat16
+I32 = mybir.dt.int32
+U32 = mybir.dt.uint32
+U16 = mybir.dt.uint16
+U8 = mybir.dt.uint8
+FP8X4 = mybir.dt.float8_e4m3fn_x4
+FP4X4 = mybir.dt.float4_e2m1fn_x4
+ALU = mybir.AluOpType
+ACT = mybir.ActivationFunctionType
+AXIS_X = mybir.AxisListType.X
+
+DY_SCALAR_COLS = 192
+
+
+def tile_attend_csqueeze_w_kernel(tc, tab_words, tab_scales, w1, steep, bias, wo, dy, js, xrows, old, offs, out):
+    nc = tc.nc
+    with ExitStack() as ctx:
+        sb = ctx.enter_context(tc.tile_pool(name="sb", bufs=1))
+        ps = ctx.enter_context(tc.psum_pool(name="ps", bufs=1))
+
+        def weave(engine_copy, dst, src):
+            engine_copy(
+                out=dst.rearrange("p (c i) t -> p c t i", i=4),
+                in_=src.rearrange("p t (c i) -> p c t i", i=4),
+            )
+
+        def quantize(name, woven):
+            width = woven.shape[1] // PACK
+            codes = sb.tile([P, width], U32, name=name + "_codes", align_bytes=64)
+            scales = sb.tile([P, width], U8, name=name + "_scales", align_bytes=64)
+            nc.vector.quantize_mx(out=codes[:].bitcast(FP8X4), scales=scales[:], in_=woven)
+            return codes[:].bitcast(FP8X4), scales[:]
+
+        offsets = sb.tile([P, J // 16], U16, name="offsets")
+        nc.sync.dma_start(out=offsets[:], in_=offs)
+
+        scale_pool = sb.tile([P, T], U8, name="scale_pool", align_bytes=64)
+        nc.vector.memset(scale_pool[:].bitcast(I32), 0)
+
+        word_pool = sb.tile([P, T], U16, name="word_pool", align_bytes=64)
+        nc.sync.dma_start(out=word_pool[:].bitcast(I32), in_=tab_words[0].bitcast(I32))
+        w1_raw = sb.tile([P, PACK, R], F32, name="w1_raw")
+        nc.sync.dma_start(out=w1_raw[:], in_=w1.rearrange("(p t) r -> p t r", t=PACK))
+        scale_rows = tab_scales[0].bitcast(I32).rearrange("(q c) n -> c q n", c=4)
+        for c in range(4):
+            nc.sync.dma_start(out=scale_pool[c:P:32, :].bitcast(I32), in_=scale_rows[c])
+        dy_raw = sb.tile([P, PACK, J], F32, name="dy_raw")
+        nc.sync.dma_start(out=dy_raw[:], in_=dy.rearrange("(p t) j -> p t j", t=PACK))
+        wo_raw = sb.tile([P, PACK, R], F32, name="wo_raw")
+        nc.sync.dma_start(out=wo_raw[:], in_=wo.rearrange("(p t) r -> p t r", t=PACK))
+        x_rows = xrows.rearrange("(p b) n -> b p n", b=PACK)
+        x_pool = []
+        for b in range(PACK):
+            x_tile = sb.tile([P, T], F32, name="x_pool%d" % b)
+            nc.sync.dma_start(out=x_tile[:], in_=x_rows[b])
+            x_pool.append(x_tile)
+        old_sb = sb.tile([P, PACK, R], F32, name="old_sb")
+        nc.sync.dma_start(out=old_sb[:], in_=old.rearrange("(p b) r -> p b r", b=PACK))
+
+        steep_sb = sb.tile([P, 1], F32, name="steep_sb")
+        nc.gpsimd.dma_start(out=steep_sb[:], in_=steep)
+        bias_sb = sb.tile([P, 1], F32, name="bias_sb")
+        nc.gpsimd.dma_start(out=bias_sb[:], in_=bias)
+        js_sb = sb.tile([P, PACK], F32, name="js_sb")
+        nc.gpsimd.dma_start(out=js_sb[:], in_=js.rearrange("o (p t) -> (o p) t", t=PACK))
+        ident = sb.tile([P, P], F32, name="ident")
+        make_identity(nc, ident[:])
+        steep_mean = sb.tile([P, 1], F32, name="steep_mean")
+        nc.gpsimd.tensor_scalar(steep_mean[:], steep_sb[:], 1.0 / GROUP, 0.0, ALU.mult, ALU.add)
+        steep_mean_neg = sb.tile([P, 1], F32, name="steep_mean_neg")
+        nc.gpsimd.tensor_scalar(steep_mean_neg[:], steep_sb[:], -1.0 / GROUP, 0.0, ALU.mult, ALU.add)
+
+        tab_codes = sb.tile([P, J], U16, name="tab_codes", align_bytes=64)
+        nc.vector.tensor_copy(out=tab_codes[:], in_=word_pool[:].indirect(offsets[:]))
+        tab_plane = sb.tile([P, J], U8, name="tab_plane", align_bytes=64)
+        nc.vector.tensor_copy(out=tab_plane[:], in_=scale_pool[:].indirect(offsets[:]))
+        w1_woven = sb.tile([P, R, PACK], BF16, name="w1_woven", align_bytes=64)
+        weave(nc.scalar.copy, w1_woven[:], w1_raw[:])
+        w1_codes, w1_plane = quantize("w1", w1_woven[:].rearrange("p r t -> p (r t)"))
+        a_ps = ps.tile([P, J], F32, name="a_ps")
+        nc.tensor.matmul_mx(out=a_ps[:], lhsT=w1_codes, lhsT_scale=w1_plane,
+                            rhs=tab_codes[:].bitcast(FP4X4), rhs_scale=tab_plane[:], start=True, stop=True)
+        a_sum = sb.tile([P, G], F32, name="a_sum")
+        nc.vector.tensor_reduce(a_sum[:], a_ps[:].rearrange("r (g i) -> r g i", i=GROUP), AXIS_X, ALU.add)
+        a_sb = sb.tile([P, J], F32, name="a_sb")
+        nc.scalar.copy(out=a_sb[:], in_=a_ps[:])
+        gate = sb.tile([P, G], F32, name="gate")
+        nc.scalar.activation(gate[:], a_sum[:], ACT.Sigmoid, bias=bias_sb[:], scale=steep_mean[:])
+
+        dy_woven = sb.tile([P, J, PACK], BF16, name="dy_woven", align_bytes=64)
+        weave(nc.scalar.copy, dy_woven[:, :DY_SCALAR_COLS, :], dy_raw[:, :, :DY_SCALAR_COLS])
+        weave(nc.vector.tensor_copy, dy_woven[:, DY_SCALAR_COLS:, :], dy_raw[:, :, DY_SCALAR_COLS:])
+        wo_woven = sb.tile([P, R, PACK], BF16, name="wo_woven", align_bytes=64)
+        weave(nc.scalar.copy, wo_woven[:], wo_raw[:])
+        dy_codes, dy_plane = quantize("dy", dy_woven[:].rearrange("p j t -> p (j t)"))
+        wo_codes, wo_plane = quantize("wo", wo_woven[:].rearrange("p r t -> p (r t)"))
+        c_ps = ps.tile([P, J], F32, name="c_ps")
+        nc.tensor.matmul_mx(out=c_ps[:], lhsT=wo_codes, lhsT_scale=wo_plane,
+                            rhs=dy_codes, rhs_scale=dy_plane, start=True, stop=True)
+
+        slope_neg = sb.tile([P, G], F32, name="slope_neg")
+        nc.vector.scalar_tensor_tensor(slope_neg[:], gate[:], 1.0, gate[:], ALU.subtract, ALU.mult)
+        prod = sb.tile([P, J], F32, name="prod")
+        nc.vector.tensor_tensor(prod[:], c_ps[:], a_sb[:], ALU.mult)
+        gated = sb.tile([P, PACK, G, 4], F32, name="gated")
+        nc.vector.tensor_tensor(
+            gated[:],
+            c_ps[:].rearrange("r (g q t) -> r t g q", q=4, t=PACK),
+            gate[:].unsqueeze(1).unsqueeze(3).broadcast_to([P, PACK, G, 4]),
+            ALU.mult,
+        )
+        dgate = sb.tile([P, G], F32, name="dgate")
+        nc.vector.tensor_reduce(dgate[:], prod[:].rearrange("r (g i) -> r g i", i=GROUP), AXIS_X, ALU.add)
+        spread = sb.tile([P, G, 4], F32, name="spread")
+        nc.vector.scalar_tensor_tensor(
+            spread[:],
+            dgate[:].unsqueeze(2).broadcast_to([P, G, 4]),
+            steep_mean_neg[:],
+            slope_neg[:].unsqueeze(2).broadcast_to([P, G, 4]),
+            ALU.mult,
+            ALU.mult,
+        )
+        da_ps = ps.tile([P, PACK, R], F32, name="da_ps")
+        for t in range(PACK):
+            nc.tensor.matmul(da_ps[:, t, :], gated[:, t].rearrange("r g q -> r (g q)"), ident[:],
+                             start=True, stop=False, is_transpose=True)
+            nc.tensor.matmul(da_ps[:, t, :], spread[:].rearrange("r g q -> r (g q)"), ident[:],
+                             start=False, stop=True, is_transpose=True)
+
+        def gather_and_turn(b):
+            picked = sb.tile([P, J], BF16, name="picked%d" % b, align_bytes=64)
+            nc.vector.tensor_copy(out=picked[:], in_=x_pool[b][:].indirect(offsets[:]))
+            pairs = picked[:].bitcast(F32)
+            turned = ps.tile([P, 2, P], F32, name="turned%d" % (b % 2))
+            for u in range(2):
+                nc.tensor.transpose(turned[:, u, :], pairs[:, u : J // 2 : 2], ident[:])
+            woven = sb.tile([P, P, 2], F32, name="x_woven%d" % b, align_bytes=64)
+            nc.scalar.copy(out=woven[:], in_=turned[:].rearrange("p u k -> p k u"))
+            return woven[:].rearrange("p k u -> p (k u)").bitcast(BF16)
+
+        x_woven = [gather_and_turn(0)]
+        g_woven = sb.tile([P, R, PACK], BF16, name="g_woven", align_bytes=64)
+        nc.vector.tensor_tensor(
+            g_woven[:],
+            da_ps[:].rearrange("p t r -> p r t"),
+            js_sb[:].unsqueeze(1).broadcast_to([P, R, PACK]),
+            ALU.mult,
+        )
+        x_woven.append(gather_and_turn(1))
+        g_codes, g_plane = quantize("g", g_woven[:].rearrange("p r t -> p (r t)"))
+
+        gw_first = ps.tile([P, PACK - 1, R], F32, name="gw_first")
+        gw_last = ps.tile([P, R], F32, name="gw_last")
+
+        def product(b):
+            x_codes, x_plane = quantize("x%d" % b, x_woven[b])
+            bank = gw_last[:] if b == PACK - 1 else gw_first[:, b, :]
+            nc.tensor.matmul_mx(out=bank, lhsT=x_codes, lhsT_scale=x_plane,
+                                rhs=g_codes, rhs_scale=g_plane, start=True, stop=True)
+
+        product(0)
+        x_woven.append(gather_and_turn(2))
+        product(1)
+        product(2)
+        x_woven.append(gather_and_turn(3))
+        out_rows = out.rearrange("(p b) r -> p b r", b=PACK)
+        res_first = sb.tile([P, PACK - 1, R], F32, name="res_first")
+        nc.vector.tensor_tensor(res_first[:], gw_first[:], old_sb[:, : PACK - 1, :], ALU.add)
+        nc.sync.dma_start(out=out_rows[:, : PACK - 1, :], in_=res_first[:])
+        product(3)
+        res_last = sb.tile([P, R], F32, name="res_last")
+        nc.vector.tensor_tensor(res_last[:], gw_last[:], old_sb[:, PACK - 1, :], ALU.add)
+        nc.sync.dma_start(out=out_rows[:, PACK - 1, :], in_=res_last[:])

@@ -30,100 +30,125 @@ def tile_attend_csqueeze_w_kernel(tc, tab_words, tab_scales, w1, steep, bias, wo
         sb = ctx.enter_context(tc.tile_pool(name="sb", bufs=1))
         ps = ctx.enter_context(tc.psum_pool(name="ps", bufs=1))
 
+        def tile(shape, dtype, name, slot=None):
+            return sb.tile(shape, dtype, name=name, tag=slot or name, align_bytes=64)
+
         def weave(engine_copy, dst, src):
             engine_copy(
                 out=dst.rearrange("p (c i) t -> p c t i", i=4),
                 in_=src.rearrange("p t (c i) -> p c t i", i=4),
             )
 
-        def quantize(name, woven):
+        def quantize(name, woven, slot=None):
             width = woven.shape[1] // PACK
-            codes = sb.tile([P, width], U32, name=name + "_codes", align_bytes=64)
-            scales = sb.tile([P, width], U8, name=name + "_scales", align_bytes=64)
+            codes = tile([P, width], U32, name + "_codes", slot)
+            scales = tile([P, width], U8, name + "_scales")
             nc.vector.quantize_mx(out=codes[:].bitcast(FP8X4), scales=scales[:], in_=woven)
             return codes[:].bitcast(FP8X4), scales[:]
 
-        offsets = sb.tile([P, J // 16], U16, name="offsets")
+        offsets = tile([P, J // 16], U16, "offsets")
         nc.sync.dma_start(out=offsets[:], in_=offs)
 
-        scale_pool = sb.tile([P, T], U8, name="scale_pool", align_bytes=64)
-        nc.vector.memset(scale_pool[:].bitcast(I32), 0)
+        scale_pool = tile([P, T], U8, "scale_pool", "slot_scale")
+        nc.gpsimd.memset(scale_pool[:].bitcast(I32), 0)
+        warm = tile([P, 1], F32, "warm")
+        nc.gpsimd.memset(warm[:], 0.0)
 
-        word_pool = sb.tile([P, T], U16, name="word_pool", align_bytes=64)
+        word_pool = tile([P, T], U16, "word_pool")
         nc.sync.dma_start(out=word_pool[:].bitcast(I32), in_=tab_words[0].bitcast(I32))
-        w1_raw = sb.tile([P, PACK, R], F32, name="w1_raw")
-        nc.sync.dma_start(out=w1_raw[:], in_=w1.rearrange("(p t) r -> p t r", t=PACK))
         scale_rows = tab_scales[0].bitcast(I32).rearrange("(q c) n -> c q n", c=4)
         for c in range(4):
             nc.sync.dma_start(out=scale_pool[c:P:32, :].bitcast(I32), in_=scale_rows[c])
-        dy_raw = sb.tile([P, PACK, J], F32, name="dy_raw")
+        warmed = tile([P, 1], F32, "warmed")
+        nc.scalar.activation(warmed[:], warm[:], ACT.Sigmoid)
+
+        w1_raw = tile([P, PACK, R], F32, "w1_raw")
+        nc.sync.dma_start(out=w1_raw[:], in_=w1.rearrange("(p t) r -> p t r", t=PACK))
+        dy_raw = tile([P, PACK, J], F32, "dy_raw")
         nc.sync.dma_start(out=dy_raw[:], in_=dy.rearrange("(p t) j -> p t j", t=PACK))
-        wo_raw = sb.tile([P, PACK, R], F32, name="wo_raw")
+        wo_raw = tile([P, PACK, R], F32, "wo_raw")
         nc.sync.dma_start(out=wo_raw[:], in_=wo.rearrange("(p t) r -> p t r", t=PACK))
+        steep_sb = tile([P, 1], F32, "steep_sb")
+        nc.sync.dma_start(out=steep_sb[:], in_=steep)
+        bias_sb = tile([P, 1], F32, "bias_sb")
+        nc.sync.dma_start(out=bias_sb[:], in_=bias)
         x_rows = xrows.rearrange("(p b) n -> b p n", b=PACK)
         x_pool = []
+        js_sb = tile([P, PACK], F32, "js_sb")
         for b in range(PACK):
-            x_tile = sb.tile([P, T], F32, name="x_pool%d" % b)
+            x_tile = tile([P, T], F32, "x_pool%d" % b)
             nc.sync.dma_start(out=x_tile[:], in_=x_rows[b])
             x_pool.append(x_tile)
-        old_sb = sb.tile([P, PACK, R], F32, name="old_sb")
+            if b == 2:
+                nc.sync.dma_start(out=js_sb[:], in_=js.rearrange("o (p t) -> (o p) t", t=PACK))
+        old_sb = tile([P, PACK, R], F32, "old_sb")
         nc.sync.dma_start(out=old_sb[:], in_=old.rearrange("(p b) r -> p b r", b=PACK))
 
-        steep_sb = sb.tile([P, 1], F32, name="steep_sb")
-        nc.gpsimd.dma_start(out=steep_sb[:], in_=steep)
-        bias_sb = sb.tile([P, 1], F32, name="bias_sb")
-        nc.gpsimd.dma_start(out=bias_sb[:], in_=bias)
-        js_sb = sb.tile([P, PACK], F32, name="js_sb")
-        nc.gpsimd.dma_start(out=js_sb[:], in_=js.rearrange("o (p t) -> (o p) t", t=PACK))
-        ident = sb.tile([P, P], F32, name="ident")
+        ident = tile([P, P], F32, "ident")
         make_identity(nc, ident[:])
-        steep_mean = sb.tile([P, 1], F32, name="steep_mean")
+        steep_mean = tile([P, 1], F32, "steep_mean")
         nc.gpsimd.tensor_scalar(steep_mean[:], steep_sb[:], 1.0 / GROUP, 0.0, ALU.mult, ALU.add)
-        steep_mean_neg = sb.tile([P, 1], F32, name="steep_mean_neg")
+        steep_mean_neg = tile([P, 1], F32, "steep_mean_neg")
         nc.gpsimd.tensor_scalar(steep_mean_neg[:], steep_sb[:], -1.0 / GROUP, 0.0, ALU.mult, ALU.add)
 
-        tab_codes = sb.tile([P, J], U16, name="tab_codes", align_bytes=64)
+        tab_codes = tile([P, J], U16, "tab_codes")
+        tab_plane = tile([P, J], U8, "tab_plane")
         nc.vector.tensor_copy(out=tab_codes[:], in_=word_pool[:].indirect(offsets[:]))
-        tab_plane = sb.tile([P, J], U8, name="tab_plane", align_bytes=64)
         nc.vector.tensor_copy(out=tab_plane[:], in_=scale_pool[:].indirect(offsets[:]))
-        w1_woven = sb.tile([P, R, PACK], BF16, name="w1_woven", align_bytes=64)
+        w1_woven = tile([P, R, PACK], BF16, "w1_woven")
         weave(nc.scalar.copy, w1_woven[:], w1_raw[:])
         w1_codes, w1_plane = quantize("w1", w1_woven[:].rearrange("p r t -> p (r t)"))
         a_ps = ps.tile([P, J], F32, name="a_ps")
         nc.tensor.matmul_mx(out=a_ps[:], lhsT=w1_codes, lhsT_scale=w1_plane,
                             rhs=tab_codes[:].bitcast(FP4X4), rhs_scale=tab_plane[:], start=True, stop=True)
-        a_sum = sb.tile([P, G], F32, name="a_sum")
-        nc.vector.tensor_reduce(a_sum[:], a_ps[:].rearrange("r (g i) -> r g i", i=GROUP), AXIS_X, ALU.add)
-        a_sb = sb.tile([P, J], F32, name="a_sb")
-        nc.scalar.copy(out=a_sb[:], in_=a_ps[:])
-        gate = sb.tile([P, G], F32, name="gate")
-        nc.scalar.activation(gate[:], a_sum[:], ACT.Sigmoid, bias=bias_sb[:], scale=steep_mean[:])
 
-        dy_woven = sb.tile([P, J, PACK], BF16, name="dy_woven", align_bytes=64)
+        dy_woven = tile([P, J, PACK], BF16, "dy_woven", "slot_scale")
         weave(nc.scalar.copy, dy_woven[:, :DY_SCALAR_COLS, :], dy_raw[:, :, :DY_SCALAR_COLS])
         weave(nc.vector.tensor_copy, dy_woven[:, DY_SCALAR_COLS:, :], dy_raw[:, :, DY_SCALAR_COLS:])
-        wo_woven = sb.tile([P, R, PACK], BF16, name="wo_woven", align_bytes=64)
+        wo_woven = tile([P, R, PACK], BF16, "wo_woven")
         weave(nc.scalar.copy, wo_woven[:], wo_raw[:])
+        a_sb = tile([P, J], F32, "a_sb", "dy_raw")
+        nc.scalar.copy(out=a_sb[:], in_=a_ps[:])
         dy_codes, dy_plane = quantize("dy", dy_woven[:].rearrange("p j t -> p (j t)"))
         wo_codes, wo_plane = quantize("wo", wo_woven[:].rearrange("p r t -> p (r t)"))
         c_ps = ps.tile([P, J], F32, name="c_ps")
         nc.tensor.matmul_mx(out=c_ps[:], lhsT=wo_codes, lhsT_scale=wo_plane,
                             rhs=dy_codes, rhs_scale=dy_plane, start=True, stop=True)
 
-        slope_neg = sb.tile([P, G], F32, name="slope_neg")
+        a_sum = tile([P, G], F32, "a_sum", "slot_scale")
+        nc.vector.tensor_reduce(a_sum[:], a_ps[:].rearrange("r (g i) -> r g i", i=GROUP), AXIS_X, ALU.add)
+        gate = tile([P, G], F32, "gate")
+        nc.scalar.activation(gate[:], a_sum[:], ACT.Sigmoid, bias=bias_sb[:], scale=steep_mean[:])
+
+        def gather_and_turn(b, woven):
+            picked = tile([P, J], BF16, "picked%d" % b)
+            if b == 0:
+                rounded = tile([P, T], BF16, "x_rounded", "slot_scale")
+                nc.scalar.activation(rounded[:], x_pool[b][:], ACT.Copy)
+                nc.scalar.activation(picked[:], rounded[:].indirect(offsets[:]), ACT.Copy)
+            else:
+                nc.vector.tensor_copy(out=picked[:], in_=x_pool[b][:].indirect(offsets[:]))
+            pairs = picked[:].bitcast(F32)
+            turned = ps.tile([P, 2, P], F32, name="turned%d" % (b % 2))
+            for u in range(2):
+                nc.tensor.transpose(turned[:, u, :], pairs[:, u : J // 2 : 2], ident[:])
+            nc.scalar.copy(out=woven.rearrange("p (k u) -> p k u", u=2), in_=turned[:].rearrange("p u k -> p k u"))
+
+        slope_neg = tile([P, G], F32, "slope_neg")
         nc.vector.scalar_tensor_tensor(slope_neg[:], gate[:], 1.0, gate[:], ALU.subtract, ALU.mult)
-        prod = sb.tile([P, J], F32, name="prod")
+
+        prod = tile([P, J], F32, "prod")
         nc.vector.tensor_tensor(prod[:], c_ps[:], a_sb[:], ALU.mult)
-        gated = sb.tile([P, PACK, G, 4], F32, name="gated")
+        gated = tile([P, PACK, G, 4], F32, "gated")
         nc.vector.tensor_tensor(
             gated[:],
             c_ps[:].rearrange("r (g q t) -> r t g q", q=4, t=PACK),
             gate[:].unsqueeze(1).unsqueeze(3).broadcast_to([P, PACK, G, 4]),
             ALU.mult,
         )
-        dgate = sb.tile([P, G], F32, name="dgate")
+        dgate = tile([P, G], F32, "dgate")
         nc.vector.tensor_reduce(dgate[:], prod[:].rearrange("r (g i) -> r g i", i=GROUP), AXIS_X, ALU.add)
-        spread = sb.tile([P, G, 4], F32, name="spread")
+        spread = tile([P, G, 4], F32, "spread")
         nc.vector.scalar_tensor_tensor(
             spread[:],
             dgate[:].unsqueeze(2).broadcast_to([P, G, 4]),
@@ -135,51 +160,47 @@ def tile_attend_csqueeze_w_kernel(tc, tab_words, tab_scales, w1, steep, bias, wo
         da_ps = ps.tile([P, PACK, R], F32, name="da_ps")
         for t in range(PACK):
             nc.tensor.matmul(da_ps[:, t, :], gated[:, t].rearrange("r g q -> r (g q)"), ident[:],
-                             start=True, stop=False, is_transpose=True)
+                             start=(t == 0), stop=False, is_transpose=True)
+        for t in range(PACK):
             nc.tensor.matmul(da_ps[:, t, :], spread[:].rearrange("r g q -> r (g q)"), ident[:],
-                             start=False, stop=True, is_transpose=True)
+                             start=False, stop=(t == PACK - 1), is_transpose=True)
 
-        def gather_and_turn(b):
-            picked = sb.tile([P, J], BF16, name="picked%d" % b, align_bytes=64)
-            nc.vector.tensor_copy(out=picked[:], in_=x_pool[b][:].indirect(offsets[:]))
-            pairs = picked[:].bitcast(F32)
-            turned = ps.tile([P, 2, P], F32, name="turned%d" % (b % 2))
-            for u in range(2):
-                nc.tensor.transpose(turned[:, u, :], pairs[:, u : J // 2 : 2], ident[:])
-            woven = sb.tile([P, P, 2], F32, name="x_woven%d" % b, align_bytes=64)
-            nc.scalar.copy(out=woven[:], in_=turned[:].rearrange("p u k -> p k u"))
-            return woven[:].rearrange("p k u -> p (k u)").bitcast(BF16)
-
-        x_woven = [gather_and_turn(0)]
-        g_woven = sb.tile([P, R, PACK], BF16, name="g_woven", align_bytes=64)
+        x01_woven = tile([P, 4 * P], F32, "x01_woven")
+        x2_woven = tile([P, 2 * P], F32, "x2_woven")
+        x3_woven = tile([P, 2 * P], F32, "x3_woven")
+        gather_and_turn(0, x01_woven[:, : 2 * P])
+        gather_and_turn(1, x01_woven[:, 2 * P :])
+        gather_and_turn(2, x2_woven[:])
+        g_woven = tile([P, R, PACK], BF16, "g_woven")
         nc.vector.tensor_tensor(
             g_woven[:],
             da_ps[:].rearrange("p t r -> p r t"),
             js_sb[:].unsqueeze(1).broadcast_to([P, R, PACK]),
             ALU.mult,
         )
-        x_woven.append(gather_and_turn(1))
         g_codes, g_plane = quantize("g", g_woven[:].rearrange("p r t -> p (r t)"))
+        gather_and_turn(3, x3_woven[:])
 
+        first_codes = tile([P, 3 * P], U32, "first_codes", "x_pool3")
+        first_plane = tile([P, 3 * P], U8, "first_plane")
+        nc.vector.quantize_mx(out=first_codes[:, : 2 * P].bitcast(FP8X4), scales=first_plane[:, : 2 * P],
+                              in_=x01_woven[:].bitcast(BF16))
+        nc.vector.quantize_mx(out=first_codes[:, 2 * P :].bitcast(FP8X4), scales=first_plane[:, 2 * P :],
+                              in_=x2_woven[:].bitcast(BF16))
         gw_first = ps.tile([P, PACK - 1, R], F32, name="gw_first")
+        for b in range(PACK - 1):
+            cols = slice(b * P, (b + 1) * P)
+            nc.tensor.matmul_mx(out=gw_first[:, b, :], lhsT=first_codes[:, cols].bitcast(FP8X4),
+                                lhsT_scale=first_plane[:, cols], rhs=g_codes, rhs_scale=g_plane,
+                                start=True, stop=True)
+        last_codes, last_plane = quantize("x3", x3_woven[:].bitcast(BF16))
         gw_last = ps.tile([P, R], F32, name="gw_last")
-
-        def product(b):
-            x_codes, x_plane = quantize("x%d" % b, x_woven[b])
-            bank = gw_last[:] if b == PACK - 1 else gw_first[:, b, :]
-            nc.tensor.matmul_mx(out=bank, lhsT=x_codes, lhsT_scale=x_plane,
-                                rhs=g_codes, rhs_scale=g_plane, start=True, stop=True)
-
-        product(0)
-        x_woven.append(gather_and_turn(2))
-        product(1)
-        product(2)
-        x_woven.append(gather_and_turn(3))
+        nc.tensor.matmul_mx(out=gw_last[:], lhsT=last_codes, lhsT_scale=last_plane,
+                            rhs=g_codes, rhs_scale=g_plane, start=True, stop=True)
         out_rows = out.rearrange("(p b) r -> p b r", b=PACK)
-        res_first = sb.tile([P, PACK - 1, R], F32, name="res_first")
+        res_first = tile([P, PACK - 1, R], F32, "res_first")
         nc.vector.tensor_tensor(res_first[:], gw_first[:], old_sb[:, : PACK - 1, :], ALU.add)
         nc.sync.dma_start(out=out_rows[:, : PACK - 1, :], in_=res_first[:])
-        product(3)
-        res_last = sb.tile([P, R], F32, name="res_last")
+        res_last = tile([P, R], F32, "res_last")
         nc.vector.tensor_tensor(res_last[:], gw_last[:], old_sb[:, PACK - 1, :], ALU.add)
         nc.sync.dma_start(out=out_rows[:, PACK - 1, :], in_=res_last[:])

@@ -51,16 +51,12 @@ def tile_attend_csqueeze_w_kernel(tc, tab_words, tab_scales, w1, steep, bias, wo
 
         scale_pool = tile([P, T], U8, "scale_pool", "slot_scale")
         nc.gpsimd.memset(scale_pool[:].bitcast(I32), 0)
-        warm = tile([P, 1], F32, "warm")
-        nc.gpsimd.memset(warm[:], 0.0)
 
         word_pool = tile([P, T], U16, "word_pool")
         nc.sync.dma_start(out=word_pool[:].bitcast(I32), in_=tab_words[0].bitcast(I32))
         scale_rows = tab_scales[0].bitcast(I32).rearrange("(q c) n -> c q n", c=4)
         for c in range(4):
             nc.sync.dma_start(out=scale_pool[c:P:32, :].bitcast(I32), in_=scale_rows[c])
-        warmed = tile([P, 1], F32, "warmed")
-        nc.scalar.activation(warmed[:], warm[:], ACT.Sigmoid)
 
         w1_raw = tile([P, PACK, R], F32, "w1_raw")
         nc.sync.dma_start(out=w1_raw[:], in_=w1.rearrange("(p t) r -> p t r", t=PACK))
@@ -86,10 +82,16 @@ def tile_attend_csqueeze_w_kernel(tc, tab_words, tab_scales, w1, steep, bias, wo
 
         ident = tile([P, P], F32, "ident")
         make_identity(nc, ident[:])
-        steep_mean = tile([P, 1], F32, "steep_mean")
-        nc.gpsimd.tensor_scalar(steep_mean[:], steep_sb[:], 1.0 / GROUP, 0.0, ALU.mult, ALU.add)
-        steep_mean_neg = tile([P, 1], F32, "steep_mean_neg")
-        nc.gpsimd.tensor_scalar(steep_mean_neg[:], steep_sb[:], -1.0 / GROUP, 0.0, ALU.mult, ALU.add)
+
+        def scaled(name, column, factor):
+            result = tile([P, 1], F32, name)
+            nc.gpsimd.tensor_scalar(result[:], column[:], factor, 0.0, ALU.mult, ALU.add)
+            return result
+
+        steep_half = scaled("steep_half", steep_sb, 0.5 / GROUP)
+        bias_half = scaled("bias_half", bias_sb, 0.5)
+        steep_quarter = scaled("steep_quarter", steep_sb, 0.25 / GROUP)
+        steep_quarter_neg = scaled("steep_quarter_neg", steep_sb, -0.25 / GROUP)
 
         tab_codes = tile([P, J], U16, "tab_codes")
         tab_plane = tile([P, J], U8, "tab_plane")
@@ -117,13 +119,19 @@ def tile_attend_csqueeze_w_kernel(tc, tab_words, tab_scales, w1, steep, bias, wo
 
         a_sum = tile([P, G], F32, "a_sum", "slot_scale")
         nc.vector.tensor_reduce(a_sum[:], a_ps[:].rearrange("r (g i) -> r g i", i=GROUP), AXIS_X, ALU.add)
+        half_tanh = tile([P, G], F32, "half_tanh")
+        nc.scalar.activation(half_tanh[:], a_sum[:], ACT.Tanh, bias=bias_half[:], scale=steep_half[:])
         gate = tile([P, G], F32, "gate")
-        nc.scalar.activation(gate[:], a_sum[:], ACT.Sigmoid, bias=bias_sb[:], scale=steep_mean[:])
+        nc.scalar.activation(gate[:], half_tanh[:], ACT.Copy, bias=0.5, scale=0.5)
+        tanh_sq = tile([P, G], F32, "tanh_sq")
+        nc.scalar.activation(tanh_sq[:], half_tanh[:], ACT.Square)
+        slope = tile([P, G], F32, "slope")
+        nc.scalar.activation(slope[:], tanh_sq[:], ACT.Identity, bias=steep_quarter[:], scale=steep_quarter_neg[:])
 
         def gather_and_turn(b, woven):
             picked = tile([P, J], BF16, "picked%d" % b)
             if b == 0:
-                rounded = tile([P, T], BF16, "x_rounded", "slot_scale")
+                rounded = tile([P, T], BF16, "x_rounded", "tanh_sq")
                 nc.scalar.activation(rounded[:], x_pool[b][:], ACT.Copy)
                 nc.scalar.activation(picked[:], rounded[:].indirect(offsets[:]), ACT.Copy)
             else:
@@ -134,8 +142,6 @@ def tile_attend_csqueeze_w_kernel(tc, tab_words, tab_scales, w1, steep, bias, wo
                 nc.tensor.transpose(turned[:, u, :], pairs[:, u : J // 2 : 2], ident[:])
             nc.scalar.copy(out=woven.rearrange("p (k u) -> p k u", u=2), in_=turned[:].rearrange("p u k -> p k u"))
 
-        slope_neg = tile([P, G], F32, "slope_neg")
-        nc.vector.scalar_tensor_tensor(slope_neg[:], gate[:], 1.0, gate[:], ALU.subtract, ALU.mult)
 
         prod = tile([P, J], F32, "prod")
         nc.vector.tensor_tensor(prod[:], c_ps[:], a_sb[:], ALU.mult)
@@ -149,12 +155,10 @@ def tile_attend_csqueeze_w_kernel(tc, tab_words, tab_scales, w1, steep, bias, wo
         dgate = tile([P, G], F32, "dgate")
         nc.vector.tensor_reduce(dgate[:], prod[:].rearrange("r (g i) -> r g i", i=GROUP), AXIS_X, ALU.add)
         spread = tile([P, G, 4], F32, "spread")
-        nc.vector.scalar_tensor_tensor(
+        nc.vector.tensor_tensor(
             spread[:],
             dgate[:].unsqueeze(2).broadcast_to([P, G, 4]),
-            steep_mean_neg[:],
-            slope_neg[:].unsqueeze(2).broadcast_to([P, G, 4]),
-            ALU.mult,
+            slope[:].unsqueeze(2).broadcast_to([P, G, 4]),
             ALU.mult,
         )
         da_ps = ps.tile([P, PACK, R], F32, name="da_ps")
@@ -181,24 +185,25 @@ def tile_attend_csqueeze_w_kernel(tc, tab_words, tab_scales, w1, steep, bias, wo
         g_codes, g_plane = quantize("g", g_woven[:].rearrange("p r t -> p (r t)"))
         gather_and_turn(3, x3_woven[:])
 
-        first_codes = tile([P, 3 * P], U32, "first_codes", "x_pool3")
+        def product(bank, codes, plane):
+            nc.tensor.matmul_mx(out=bank, lhsT=codes, lhsT_scale=plane, rhs=g_codes, rhs_scale=g_plane,
+                                start=True, stop=True)
+
+        first_words = tile([P, 3 * P], U32, "first_words", "x_pool3")
         first_plane = tile([P, 3 * P], U8, "first_plane")
-        nc.vector.quantize_mx(out=first_codes[:, : 2 * P].bitcast(FP8X4), scales=first_plane[:, : 2 * P],
+        first_codes = first_words[:].bitcast(FP8X4)
+        nc.vector.quantize_mx(out=first_codes[:, : 2 * P], scales=first_plane[:, : 2 * P],
                               in_=x01_woven[:].bitcast(BF16))
-        nc.vector.quantize_mx(out=first_codes[:, 2 * P :].bitcast(FP8X4), scales=first_plane[:, 2 * P :],
+        nc.vector.quantize_mx(out=first_codes[:, 2 * P :], scales=first_plane[:, 2 * P :],
                               in_=x2_woven[:].bitcast(BF16))
         gw_first = ps.tile([P, PACK - 1, R], F32, name="gw_first")
         for b in range(PACK - 1):
             cols = slice(b * P, (b + 1) * P)
-            nc.tensor.matmul_mx(out=gw_first[:, b, :], lhsT=first_codes[:, cols].bitcast(FP8X4),
-                                lhsT_scale=first_plane[:, cols], rhs=g_codes, rhs_scale=g_plane,
-                                start=True, stop=True)
-        last_codes, last_plane = quantize("x3", x3_woven[:].bitcast(BF16))
+            product(gw_first[:, b, :], first_codes[:, cols], first_plane[:, cols])
         gw_last = ps.tile([P, R], F32, name="gw_last")
-        nc.tensor.matmul_mx(out=gw_last[:], lhsT=last_codes, lhsT_scale=last_plane,
-                            rhs=g_codes, rhs_scale=g_plane, start=True, stop=True)
+        product(gw_last[:], *quantize("x3", x3_woven[:].bitcast(BF16)))
         out_rows = out.rearrange("(p b) r -> p b r", b=PACK)
-        res_first = tile([P, PACK - 1, R], F32, "res_first")
+        res_first = tile([P, PACK - 1, R], F32, "res_first", "x3_woven")
         nc.vector.tensor_tensor(res_first[:], gw_first[:], old_sb[:, : PACK - 1, :], ALU.add)
         nc.sync.dma_start(out=out_rows[:, : PACK - 1, :], in_=res_first[:])
         res_last = tile([P, R], F32, "res_last")

@@ -108,14 +108,18 @@ def tile_attend_csqueeze_w_kernel(tc, tab_words, tab_scales, w1, steep, bias, wo
         weave(nc.scalar.copy, dy_woven[:, :DY_SCALAR_COLS, :], dy_raw[:, :, :DY_SCALAR_COLS])
         weave(nc.vector.tensor_copy, dy_woven[:, DY_SCALAR_COLS:, :], dy_raw[:, :, DY_SCALAR_COLS:])
         wo_woven = tile([P, R, PACK], BF16, "wo_woven")
-        weave(nc.scalar.copy, wo_woven[:], wo_raw[:])
+        weave(nc.vector.tensor_copy, wo_woven[:], wo_raw[:])
         a_sb = tile([P, J], F32, "a_sb", "dy_raw")
         nc.scalar.copy(out=a_sb[:], in_=a_ps[:])
-        dy_codes, dy_plane = quantize("dy", dy_woven[:].rearrange("p j t -> p (j t)"))
+        half = J // 2
+        hi_codes, hi_plane = quantize("dy_hi", dy_woven[:, half:, :].rearrange("p j t -> p (j t)"))
         wo_codes, wo_plane = quantize("wo", wo_woven[:].rearrange("p r t -> p (r t)"))
+        lo_codes, lo_plane = quantize("dy_lo", dy_woven[:, :half, :].rearrange("p j t -> p (j t)"))
         c_ps = ps.tile([P, J], F32, name="c_ps")
-        nc.tensor.matmul_mx(out=c_ps[:], lhsT=wo_codes, lhsT_scale=wo_plane,
-                            rhs=dy_codes, rhs_scale=dy_plane, start=True, stop=True)
+        nc.tensor.matmul_mx(out=c_ps[:, half:], lhsT=wo_codes, lhsT_scale=wo_plane,
+                            rhs=hi_codes, rhs_scale=hi_plane, start=True, stop=True)
+        nc.tensor.matmul_mx(out=c_ps[:, :half], lhsT=wo_codes, lhsT_scale=wo_plane,
+                            rhs=lo_codes, rhs_scale=lo_plane, start=True, stop=True)
 
         a_sum = tile([P, G], F32, "a_sum", "slot_scale")
         nc.vector.tensor_reduce(a_sum[:], a_ps[:].rearrange("r (g i) -> r g i", i=GROUP), AXIS_X, ALU.add)
@@ -169,41 +173,32 @@ def tile_attend_csqueeze_w_kernel(tc, tab_words, tab_scales, w1, steep, bias, wo
             nc.tensor.matmul(da_ps[:, t, :], spread[:].rearrange("r g q -> r (g q)"), ident[:],
                              start=False, stop=(t == PACK - 1), is_transpose=True)
 
-        x01_woven = tile([P, 4 * P], F32, "x01_woven")
-        x2_woven = tile([P, 2 * P], F32, "x2_woven")
-        x3_woven = tile([P, 2 * P], F32, "x3_woven")
-        gather_and_turn(0, x01_woven[:, : 2 * P])
-        gather_and_turn(1, x01_woven[:, 2 * P :])
-        gather_and_turn(2, x2_woven[:])
-        g_woven = tile([P, R, PACK], BF16, "g_woven")
+        first_woven = tile([P, PACK, 2 * P], F32, "first_woven")
+        last_woven = tile([P, 2 * P], F32, "last_woven")
+        for b in range(PACK - 1):
+            gather_and_turn(b, first_woven[:, 1 + b, :])
         nc.vector.tensor_tensor(
-            g_woven[:],
+            first_woven[:, 0, :].bitcast(BF16).rearrange("p (r t) -> p r t", t=PACK),
             da_ps[:].rearrange("p t r -> p r t"),
             js_sb[:].unsqueeze(1).broadcast_to([P, R, PACK]),
             ALU.mult,
         )
-        g_codes, g_plane = quantize("g", g_woven[:].rearrange("p r t -> p (r t)"))
-        gather_and_turn(3, x3_woven[:])
+        gather_and_turn(PACK - 1, last_woven[:])
+        first_codes, first_plane = quantize(
+            "first", first_woven[:].rearrange("p a w -> p (a w)").bitcast(BF16), "x_pool3")
 
         def product(bank, codes, plane):
-            nc.tensor.matmul_mx(out=bank, lhsT=codes, lhsT_scale=plane, rhs=g_codes, rhs_scale=g_plane,
-                                start=True, stop=True)
+            nc.tensor.matmul_mx(out=bank, lhsT=codes, lhsT_scale=plane, rhs=first_codes[:, :R],
+                                rhs_scale=first_plane[:, :R], start=True, stop=True)
 
-        first_words = tile([P, 3 * P], U32, "first_words", "x_pool3")
-        first_plane = tile([P, 3 * P], U8, "first_plane")
-        first_codes = first_words[:].bitcast(FP8X4)
-        nc.vector.quantize_mx(out=first_codes[:, : 2 * P], scales=first_plane[:, : 2 * P],
-                              in_=x01_woven[:].bitcast(BF16))
-        nc.vector.quantize_mx(out=first_codes[:, 2 * P :], scales=first_plane[:, 2 * P :],
-                              in_=x2_woven[:].bitcast(BF16))
         gw_first = ps.tile([P, PACK - 1, R], F32, name="gw_first")
         for b in range(PACK - 1):
-            cols = slice(b * P, (b + 1) * P)
+            cols = slice((1 + b) * P, (2 + b) * P)
             product(gw_first[:, b, :], first_codes[:, cols], first_plane[:, cols])
         gw_last = ps.tile([P, R], F32, name="gw_last")
-        product(gw_last[:], *quantize("x3", x3_woven[:].bitcast(BF16)))
+        product(gw_last[:], *quantize("last", last_woven[:].bitcast(BF16)))
         out_rows = out.rearrange("(p b) r -> p b r", b=PACK)
-        res_first = tile([P, PACK - 1, R], F32, "res_first", "x3_woven")
+        res_first = tile([P, PACK - 1, R], F32, "res_first", "last_woven")
         nc.vector.tensor_tensor(res_first[:], gw_first[:], old_sb[:, : PACK - 1, :], ALU.add)
         nc.sync.dma_start(out=out_rows[:, : PACK - 1, :], in_=res_first[:])
         res_last = tile([P, R], F32, "res_last")

@@ -64,34 +64,26 @@ def tile_attend_csqueeze_w_kernel(tc, tab_words, tab_scales, w1, steep, bias, wo
         nc.sync.dma_start(out=dy_raw[:], in_=dy.rearrange("(p t) j -> p t j", t=PACK))
         wo_raw = tile([P, PACK, R], F32, "wo_raw")
         nc.sync.dma_start(out=wo_raw[:], in_=wo.rearrange("(p t) r -> p t r", t=PACK))
-        steep_sb = tile([P, 1], F32, "steep_sb")
-        nc.sync.dma_start(out=steep_sb[:], in_=steep)
-        bias_sb = tile([P, 1], F32, "bias_sb")
-        nc.sync.dma_start(out=bias_sb[:], in_=bias)
+        gate_rows = tile([P, R], F32, "gate_rows")
+        nc.gpsimd.memset(gate_rows[:], 0.0)
+        nc.sync.dma_start(out=gate_rows[0:1, :], in_=steep.rearrange("r o -> o r"))
+        nc.sync.dma_start(out=gate_rows[1:2, :], in_=bias.rearrange("r o -> o r"))
         x_rows = xrows.rearrange("(p b) n -> b p n", b=PACK)
         x_pool = []
-        js_sb = tile([P, PACK], F32, "js_sb")
+        js_row = tile([P, J], F32, "js_row")
+        nc.gpsimd.memset(js_row[:], 0.0)
         for b in range(PACK):
             x_tile = tile([P, T], F32, "x_pool%d" % b)
             nc.sync.dma_start(out=x_tile[:], in_=x_rows[b])
             x_pool.append(x_tile)
-            if b == 2:
-                nc.sync.dma_start(out=js_sb[:], in_=js.rearrange("o (p t) -> (o p) t", t=PACK))
+            if b == 0:
+                nc.sync.dma_start(out=js_row[0:1, :], in_=js)
         old_sb = tile([P, PACK, R], F32, "old_sb")
         nc.sync.dma_start(out=old_sb[:], in_=old.rearrange("(p b) r -> p b r", b=PACK))
 
         ident = tile([P, P], F32, "ident")
         make_identity(nc, ident[:])
 
-        def scaled(name, column, factor):
-            result = tile([P, 1], F32, name)
-            nc.gpsimd.tensor_scalar(result[:], column[:], factor, 0.0, ALU.mult, ALU.add)
-            return result
-
-        steep_half = scaled("steep_half", steep_sb, 0.5 / GROUP)
-        bias_half = scaled("bias_half", bias_sb, 0.5)
-        steep_quarter = scaled("steep_quarter", steep_sb, 0.25 / GROUP)
-        steep_quarter_neg = scaled("steep_quarter_neg", steep_sb, -0.25 / GROUP)
 
         tab_codes = tile([P, J], U16, "tab_codes")
         tab_plane = tile([P, J], U8, "tab_plane")
@@ -111,6 +103,19 @@ def tile_attend_csqueeze_w_kernel(tc, tab_words, tab_scales, w1, steep, bias, wo
         weave(nc.vector.tensor_copy, wo_woven[:], wo_raw[:])
         a_sb = tile([P, J], F32, "a_sb", "dy_raw")
         nc.scalar.copy(out=a_sb[:], in_=a_ps[:])
+        gate_cols = ps.tile([P, P], F32, name="gate_cols", tag="gw_last")
+        nc.tensor.transpose(gate_cols[:], gate_rows[:], ident[:])
+
+        def scaled(name, column, factor):
+            result = tile([P, 1], F32, name)
+            nc.scalar.activation(result[:], gate_cols[:, column : column + 1], ACT.Copy, scale=factor)
+            return result
+
+        steep_half = scaled("steep_half", 0, 0.5 / GROUP)
+        bias_half = scaled("bias_half", 1, 0.5)
+        steep_quarter = scaled("steep_quarter", 0, 0.25 / GROUP)
+        steep_quarter_neg = scaled("steep_quarter_neg", 0, -0.25 / GROUP)
+
         half = J // 2
         hi_codes, hi_plane = quantize("dy_hi", dy_woven[:, half:, :].rearrange("p j t -> p (j t)"))
         wo_codes, wo_plane = quantize("wo", wo_woven[:].rearrange("p r t -> p (r t)"))
@@ -147,6 +152,10 @@ def tile_attend_csqueeze_w_kernel(tc, tab_words, tab_scales, w1, steep, bias, wo
             nc.scalar.copy(out=woven.rearrange("p (k u) -> p k u", u=2), in_=turned[:].rearrange("p u k -> p k u"))
 
 
+        js_cols = ps.tile([P, PACK, P], F32, name="js_cols")
+        for t in range(PACK):
+            nc.tensor.transpose(js_cols[:, t, :], js_row[:, t:J:PACK], ident[:])
+
         prod = tile([P, J], F32, "prod")
         nc.vector.tensor_tensor(prod[:], c_ps[:], a_sb[:], ALU.mult)
         gated = tile([P, PACK, G, 4], F32, "gated")
@@ -175,15 +184,18 @@ def tile_attend_csqueeze_w_kernel(tc, tab_words, tab_scales, w1, steep, bias, wo
 
         first_woven = tile([P, PACK, 2 * P], F32, "first_woven")
         last_woven = tile([P, 2 * P], F32, "last_woven")
-        for b in range(PACK - 1):
-            gather_and_turn(b, first_woven[:, 1 + b, :])
+        gather_and_turn(0, first_woven[:, 1, :])
+        gather_and_turn(1, first_woven[:, 2, :])
+        js_sb = tile([P, PACK], F32, "js_sb", "x_pool1")
+        nc.vector.tensor_copy(out=js_sb[:], in_=js_cols[:, :, 0])
         nc.vector.tensor_tensor(
             first_woven[:, 0, :].bitcast(BF16).rearrange("p (r t) -> p r t", t=PACK),
             da_ps[:].rearrange("p t r -> p r t"),
             js_sb[:].unsqueeze(1).broadcast_to([P, R, PACK]),
             ALU.mult,
         )
-        gather_and_turn(PACK - 1, last_woven[:])
+        gather_and_turn(2, first_woven[:, 3, :])
+        gather_and_turn(3, last_woven[:])
         first_codes, first_plane = quantize(
             "first", first_woven[:].rearrange("p a w -> p (a w)").bitcast(BF16), "x_pool3")
 

from contextlib import ExitStack

import concourse.mybir as mybir
from concourse.masks import make_identity

K, R, F, T, J, G = 512, 128, 512, 2048, 512, 32
P = 128
PACK = 4
GROUP = J // G
FLOPS = 2 * R * J * K + 2 * R * J * F + 2 * K * R * J

F32 = mybir.dt.float32
BF16 = mybir.dt.bfloat16
I32 = mybir.dt.int32
U32 = mybir.dt.uint32
U16 = mybir.dt.uint16
U8 = mybir.dt.uint8
FP8X4 = mybir.dt.float8_e4m3fn_x4
FP4X4 = mybir.dt.float4_e2m1fn_x4
ALU = mybir.AluOpType
ACT = mybir.ActivationFunctionType
AXIS_X = mybir.AxisListType.X

DY_SCALAR_COLS = 192


def tile_attend_csqueeze_w_kernel(tc, tab_words, tab_scales, w1, steep, bias, wo, dy, js, xrows, old, offs, out):
    nc = tc.nc
    with ExitStack() as ctx:
        sb = ctx.enter_context(tc.tile_pool(name="sb", bufs=1))
        ps = ctx.enter_context(tc.psum_pool(name="ps", bufs=1))

        def tile(shape, dtype, name, slot=None):
            return sb.tile(shape, dtype, name=name, tag=slot or name, align_bytes=64)

        def weave(engine_copy, dst, src):
            engine_copy(
                out=dst.rearrange("p (c i) t -> p c t i", i=4),
                in_=src.rearrange("p t (c i) -> p c t i", i=4),
            )

        def quantize(name, woven, slot=None):
            width = woven.shape[1] // PACK
            codes = tile([P, width], U32, name + "_codes", slot)
            scales = tile([P, width], U8, name + "_scales")
            nc.vector.quantize_mx(out=codes[:].bitcast(FP8X4), scales=scales[:], in_=woven)
            return codes[:].bitcast(FP8X4), scales[:]

        offsets = tile([P, J // 16], U16, "offsets")
        nc.sync.dma_start(out=offsets[:], in_=offs)

        scale_pool = tile([P, T], U8, "scale_pool", "slot_scale")
        nc.gpsimd.memset(scale_pool[:].bitcast(I32), 0)

        word_pool = tile([P, T], U16, "word_pool")
        nc.sync.dma_start(out=word_pool[:].bitcast(I32), in_=tab_words[0].bitcast(I32))
        scale_rows = tab_scales[0].bitcast(I32).rearrange("(q c) n -> c q n", c=4)
        for c in range(4):
            nc.sync.dma_start(out=scale_pool[c:P:32, :].bitcast(I32), in_=scale_rows[c])

        w1_raw = tile([P, PACK, R], F32, "w1_raw")
        nc.sync.dma_start(out=w1_raw[:], in_=w1.rearrange("(p t) r -> p t r", t=PACK))
        dy_raw = tile([P, PACK, J], F32, "dy_raw")
        nc.sync.dma_start(out=dy_raw[:], in_=dy.rearrange("(p t) j -> p t j", t=PACK))
        wo_raw = tile([P, PACK, R], F32, "wo_raw")
        nc.sync.dma_start(out=wo_raw[:], in_=wo.rearrange("(p t) r -> p t r", t=PACK))
        gate_rows = tile([P, R], F32, "gate_rows")
        nc.gpsimd.memset(gate_rows[:], 0.0)
        nc.sync.dma_start(out=gate_rows[0:1, :], in_=steep.rearrange("r o -> o r"))
        nc.sync.dma_start(out=gate_rows[1:2, :], in_=bias.rearrange("r o -> o r"))
        x_rows = xrows.rearrange("(p b) n -> b p n", b=PACK)
        x_pool = []
        js_row = tile([P, J], F32, "js_row")
        nc.gpsimd.memset(js_row[:], 0.0)
        for b in range(PACK):
            x_tile = tile([P, T], F32, "x_pool%d" % b)
            nc.sync.dma_start(out=x_tile[:], in_=x_rows[b])
            x_pool.append(x_tile)
            if b == 0:
                nc.sync.dma_start(out=js_row[0:1, :], in_=js)
        old_sb = tile([P, PACK, R], F32, "old_sb")
        nc.sync.dma_start(out=old_sb[:], in_=old.rearrange("(p b) r -> p b r", b=PACK))

        ident = tile([P, P], F32, "ident")
        make_identity(nc, ident[:])


        tab_codes = tile([P, J], U16, "tab_codes")
        tab_plane = tile([P, J], U8, "tab_plane")
        nc.vector.tensor_copy(out=tab_codes[:], in_=word_pool[:].indirect(offsets[:]))
        nc.vector.tensor_copy(out=tab_plane[:], in_=scale_pool[:].indirect(offsets[:]))
        w1_woven = tile([P, R, PACK], BF16, "w1_woven")
        weave(nc.scalar.copy, w1_woven[:], w1_raw[:])
        w1_codes, w1_plane = quantize("w1", w1_woven[:].rearrange("p r t -> p (r t)"))
        a_ps = ps.tile([P, J], F32, name="a_ps")
        nc.tensor.matmul_mx(out=a_ps[:], lhsT=w1_codes, lhsT_scale=w1_plane,
                            rhs=tab_codes[:].bitcast(FP4X4), rhs_scale=tab_plane[:], start=True, stop=True)

        dy_woven = tile([P, J, PACK], BF16, "dy_woven", "slot_scale")
        weave(nc.scalar.copy, dy_woven[:, :DY_SCALAR_COLS, :], dy_raw[:, :, :DY_SCALAR_COLS])
        weave(nc.vector.tensor_copy, dy_woven[:, DY_SCALAR_COLS:, :], dy_raw[:, :, DY_SCALAR_COLS:])
        wo_woven = tile([P, R, PACK], BF16, "wo_woven")
        weave(nc.vector.tensor_copy, wo_woven[:], wo_raw[:])
        a_sb = tile([P, J], F32, "a_sb", "dy_raw")
        nc.scalar.copy(out=a_sb[:], in_=a_ps[:])
        gate_cols = ps.tile([P, P], F32, name="gate_cols", tag="gw_last")
        nc.tensor.transpose(gate_cols[:], gate_rows[:], ident[:])

        def scaled(name, column, factor):
            result = tile([P, 1], F32, name)
            nc.scalar.activation(result[:], gate_cols[:, column : column + 1], ACT.Copy, scale=factor)
            return result

        steep_half = scaled("steep_half", 0, 0.5 / GROUP)
        bias_half = scaled("bias_half", 1, 0.5)
        steep_quarter = scaled("steep_quarter", 0, 0.25 / GROUP)
        steep_quarter_neg = scaled("steep_quarter_neg", 0, -0.25 / GROUP)

        half = J // 2
        hi_codes, hi_plane = quantize("dy_hi", dy_woven[:, half:, :].rearrange("p j t -> p (j t)"))
        wo_codes, wo_plane = quantize("wo", wo_woven[:].rearrange("p r t -> p (r t)"))
        lo_codes, lo_plane = quantize("dy_lo", dy_woven[:, :half, :].rearrange("p j t -> p (j t)"))
        c_ps = ps.tile([P, J], F32, name="c_ps")
        nc.tensor.matmul_mx(out=c_ps[:, half:], lhsT=wo_codes, lhsT_scale=wo_plane,
                            rhs=hi_codes, rhs_scale=hi_plane, start=True, stop=True)
        nc.tensor.matmul_mx(out=c_ps[:, :half], lhsT=wo_codes, lhsT_scale=wo_plane,
                            rhs=lo_codes, rhs_scale=lo_plane, start=True, stop=True)

        a_sum = tile([P, G], F32, "a_sum", "slot_scale")
        nc.vector.tensor_reduce(a_sum[:], a_ps[:].rearrange("r (g i) -> r g i", i=GROUP), AXIS_X, ALU.add)
        half_tanh = tile([P, G], F32, "half_tanh")
        nc.scalar.activation(half_tanh[:], a_sum[:], ACT.Tanh, bias=bias_half[:], scale=steep_half[:])
        gate = tile([P, G], F32, "gate")
        nc.scalar.activation(gate[:], half_tanh[:], ACT.Copy, bias=0.5, scale=0.5)
        tanh_sq = tile([P, G], F32, "tanh_sq")
        nc.scalar.activation(tanh_sq[:], half_tanh[:], ACT.Square)
        slope = tile([P, G], F32, "slope")
        nc.scalar.activation(slope[:], tanh_sq[:], ACT.Identity, bias=steep_quarter[:], scale=steep_quarter_neg[:])

        def gather_and_turn(b, woven):
            picked = tile([P, J], BF16, "picked%d" % b)
            if b == 0:
                rounded = tile([P, T], BF16, "x_rounded", "tanh_sq")
                nc.scalar.activation(rounded[:], x_pool[b][:], ACT.Copy)
                nc.scalar.activation(picked[:], rounded[:].indirect(offsets[:]), ACT.Copy)
            else:
                nc.vector.tensor_copy(out=picked[:], in_=x_pool[b][:].indirect(offsets[:]))
            pairs = picked[:].bitcast(F32)
            turned = ps.tile([P, 2, P], F32, name="turned%d" % (b % 2))
            for u in range(2):
                nc.tensor.transpose(turned[:, u, :], pairs[:, u : J // 2 : 2], ident[:])
            nc.scalar.copy(out=woven.rearrange("p (k u) -> p k u", u=2), in_=turned[:].rearrange("p u k -> p k u"))


        js_cols = ps.tile([P, PACK, P], F32, name="js_cols")
        for t in range(PACK):
            nc.tensor.transpose(js_cols[:, t, :], js_row[:, t:J:PACK], ident[:])

        prod = tile([P, J], F32, "prod")
        nc.vector.tensor_tensor(prod[:], c_ps[:], a_sb[:], ALU.mult)
        gated = tile([P, PACK, G, 4], F32, "gated")
        nc.vector.tensor_tensor(
            gated[:],
            c_ps[:].rearrange("r (g q t) -> r t g q", q=4, t=PACK),
            gate[:].unsqueeze(1).unsqueeze(3).broadcast_to([P, PACK, G, 4]),
            ALU.mult,
        )
        dgate = tile([P, G], F32, "dgate")
        nc.vector.tensor_reduce(dgate[:], prod[:].rearrange("r (g i) -> r g i", i=GROUP), AXIS_X, ALU.add)
        spread = tile([P, G, 4], F32, "spread")
        nc.vector.tensor_tensor(
            spread[:],
            dgate[:].unsqueeze(2).broadcast_to([P, G, 4]),
            slope[:].unsqueeze(2).broadcast_to([P, G, 4]),
            ALU.mult,
        )
        da_ps = ps.tile([P, PACK, R], F32, name="da_ps")
        for t in range(PACK):
            nc.tensor.matmul(da_ps[:, t, :], gated[:, t].rearrange("r g q -> r (g q)"), ident[:],
                             start=(t == 0), stop=False, is_transpose=True)
        for t in range(PACK):
            nc.tensor.matmul(da_ps[:, t, :], spread[:].rearrange("r g q -> r (g q)"), ident[:],
                             start=False, stop=(t == PACK - 1), is_transpose=True)

        first_woven = tile([P, PACK, 2 * P], F32, "first_woven")
        last_woven = tile([P, 2 * P], F32, "last_woven")
        gather_and_turn(0, first_woven[:, 1, :])
        gather_and_turn(1, first_woven[:, 2, :])
        js_sb = tile([P, PACK], F32, "js_sb", "x_pool1")
        nc.vector.tensor_copy(out=js_sb[:], in_=js_cols[:, :, 0])
        nc.vector.tensor_tensor(
            first_woven[:, 0, :].bitcast(BF16).rearrange("p (r t) -> p r t", t=PACK),
            da_ps[:].rearrange("p t r -> p r t"),
            js_sb[:].unsqueeze(1).broadcast_to([P, R, PACK]),
            ALU.mult,
        )
        gather_and_turn(2, first_woven[:, 3, :])
        gather_and_turn(3, last_woven[:])
        first_codes, first_plane = quantize(
            "first", first_woven[:].rearrange("p a w -> p (a w)").bitcast(BF16), "x_pool3")

        def product(bank, codes, plane):
            nc.tensor.matmul_mx(out=bank, lhsT=codes, lhsT_scale=plane, rhs=first_codes[:, :R],
                                rhs_scale=first_plane[:, :R], start=True, stop=True)

        gw_first = ps.tile([P, PACK - 1, R], F32, name="gw_first")
        for b in range(PACK - 1):
            cols = slice((1 + b) * P, (2 + b) * P)
            product(gw_first[:, b, :], first_codes[:, cols], first_plane[:, cols])
        gw_last = ps.tile([P, R], F32, name="gw_last")
        product(gw_last[:], *quantize("last", last_woven[:].bitcast(BF16)))
        out_rows = out.rearrange("(p b) r -> p b r", b=PACK)
        res_first = tile([P, PACK - 1, R], F32, "res_first", "last_woven")
        nc.vector.tensor_tensor(res_first[:], gw_first[:], old_sb[:, : PACK - 1, :], ALU.add)
        nc.sync.dma_start(out=out_rows[:, : PACK - 1, :], in_=res_first[:])
        res_last = tile([P, R], F32, "res_last")
        nc.vector.tensor_tensor(res_last[:], gw_last[:], old_sb[:, PACK - 1, :], ALU.add)
        nc.sync.dma_start(out=out_rows[:, PACK - 1, :], in_=res_last[:])
